import numpy as np
import ml_dtypes


def mxq(x, axis, fmt="e4m3"):
    dtype, down = {"e4m3": (ml_dtypes.float8_e4m3fn, 7), "e5m2": (ml_dtypes.float8_e5m2, 14)}[fmt]
    v = np.moveaxis(np.asarray(x, np.float32).astype(ml_dtypes.bfloat16).astype(np.float64), axis, -1)
    blocks = v.reshape(v.shape[:-1] + (-1, 32))
    amax = np.abs(blocks).max(-1, keepdims=True)
    byte = np.maximum(np.where(amax > 0, np.frexp(amax)[1] - 1 + 127, 0) - down, 1)
    scale = np.exp2(byte - 127.0)
    codes = (blocks / scale).astype(np.float32).astype(dtype).astype(np.float64)
    return np.moveaxis((codes * scale).reshape(v.shape), -1, axis)


WIDE = False


def mx_kscale(k):
    if not WIDE:
        return np.ones(k)
    levels = np.array([18, -18])
    if k % 512:
        return np.exp2(np.random.permutation(np.resize(levels, k // 32))).repeat(32)
    a = np.empty((k // 512, 16))
    for p in range(k // 512):
        a[p, :8] = np.random.permutation(np.resize(levels, 8))
        for g in range(8):
            far = levels[np.abs(levels - a[p, g]) >= 10]
            a[p, g + 8] = far[np.random.randint(len(far))]
    return np.exp2(a.ravel()).repeat(32)


def f64(x):
    return np.asarray(x).astype(np.float64)


def striped(idx):
    return np.tile(np.asarray(idx).reshape(-1, 16).T, (8, 1)).astype(np.uint16)


def unstriped(offs):
    return offs[:16].T.reshape(-1).astype(np.int64)


def setup_inputs():
    n = np.random.standard_normal
    uni = np.random.uniform
    qi = np.random.permutation(2048)[:512]
    idx = np.random.permutation(2048)[:512]
    f_d = mx_kscale(512)
    f_e = mx_kscale(512)
    f_i = np.ones(2048)
    f_i[idx] = mx_kscale(512)
    f_j = np.ones(2048)
    f_j[qi] = mx_kscale(512)
    return {
        "qT": (0.5 * n((512, 2048)) * f_d[:, None] * f_j[None, :]).astype(np.float32),
        "kT": (n((512, 2048)) / np.sqrt(512) / f_d[:, None] * f_i[None, :]).astype(np.float32),
        "doT": (n((512, 2048)) * f_e[:, None]).astype(np.float32),
        "vT": (n((512, 2048)) / np.sqrt(512) / f_e[:, None]).astype(np.float32),
        "sq_": np.tile(uni(0.75, 1.3, 2048) / f_j, (128, 1)).astype(np.float32),
        "ts": np.tile(uni(0.75, 1.3, 2048) / f_i, (128, 1)).astype(np.float32),
        "lse": np.tile(np.log(512) + 0.1 + 0.1 * n(2048), (128, 1)).astype(np.float32),
        "dl": np.tile(0.3 * n(2048), (128, 1)).astype(np.float32),
        "wq": np.tile(uni(0.75, 1.3, 2048), (128, 1)).astype(np.float32),
        "qoffs": striped(qi),
        "offs": striped(idx),
    }


def reference(qT, kT, doT, vT, sq_, ts, lse, dl, wq, qoffs, offs):
    qi = unstriped(qoffs)
    idx = unstriped(offs)
    q = f64(qT)[:, qi]
    k = f64(kT)[:, idx]
    do = f64(doT)[:, qi]
    vT_i = f64(vT)[:, idx]
    sj = f64(sq_)[:1][:, qi]
    sc = sj.T
    ts_i = f64(ts)[:1][:, idx]
    lj = f64(lse)[:1][:, qi]
    lc = lj.T
    dj = f64(dl)[:1][:, qi]
    dc = dj.T
    wj = f64(wq)[:1][:, qi]
    wc = wj.T
    a = mxq(q, 0, "e4m3").T @ mxq(k, 0, "e4m3")
    p = np.exp(sc * ts_i * a - lc)
    dp = mxq(do, 0, "e5m2").T @ mxq(vT_i, 0, "e4m3")
    g = wc * sc * ts_i * p * (dp - dc)
    dq = mxq(k, 1, "e4m3") @ mxq(g, 1, "e5m2").T
    dk = mxq(q, 1, "e4m3") @ mxq(g, 0, "e5m2")
    out_0 = np.zeros((512, 2048))
    out_0[:, qi] = dq
    out_1 = np.zeros((512, 2048))
    out_1[:, idx] = dk
    return out_0, out_1

@@ -1,0 +1,258 @@
+from contextlib import ExitStack
+
+import concourse.mybir as mybir
+from concourse.masks import make_identity
+
+D, SLOTS, POOL = 512, 512, 2048
+FLOPS = 4 * 2 * 512 * 512 * 512
+BYTES = 6 * D * POOL * 4 + 5 * POOL * 4 + 2 * 128 * 32 * 2
+
+F32 = mybir.dt.float32
+BF16 = mybir.dt.bfloat16
+U32 = mybir.dt.uint32
+U16 = mybir.dt.uint16
+U8 = mybir.dt.uint8
+E4M3 = mybir.dt.float8_e4m3fn_x4
+E5M2 = mybir.dt.float8_e5m2_x4
+ACT = mybir.ActivationFunctionType
+ALU = mybir.AluOpType
+
+P = 128
+PACK = 4
+RING = 7
+Q, K, DO, V = range(4)
+
+
+def tile_attend_gclatt_qk_kernel(
+    tc, qT, kT, doT, vT, sq_, ts, lse, dl, wq, qoffs, offs, out_0, out_1
+):
+    nc = tc.nc
+    with ExitStack() as ctx:
+        keep = ctx.enter_context(tc.tile_pool(name="keep", bufs=1))
+        planes = ctx.enter_context(tc.tile_pool(name="planes", bufs=1))
+        woven = ctx.enter_context(tc.tile_pool(name="woven", bufs=3))
+        pairs = ctx.enter_context(tc.tile_pool(name="pairs", bufs=4))
+        staged = ctx.enter_context(tc.tile_pool(name="staged", bufs=4))
+        psum = ctx.enter_context(tc.psum_pool(name="psum", bufs=8))
+
+        def bank():
+            return psum.tile([P, SLOTS], F32, name="bank")
+
+        q_list = keep.tile([P, SLOTS // 16], U16, name="q_list")
+        k_list = keep.tile([P, SLOTS // 16], U16, name="k_list")
+
+        def slot_of(src_nr, t):
+            return "slot%d" % ((PACK * src_nr + t) % RING)
+
+        def load_plane(src_nr, t):
+            src = (qT, kT, doT, vT)[src_nr]
+            plane = planes.tile([P, POOL], F32, name="plane", tag=slot_of(src_nr, t))
+            nc.sync.dma_start(out=plane[:], in_=src.rearrange("(p t) n -> t p n", t=PACK)[t])
+            return plane
+
+        def gather_plane(dst, plane, slot_list):
+            nc.vector.tensor_copy(out=dst, in_=plane[:].indirect(slot_list[:]))
+
+        def quantize(name, src, fmt, tag=None):
+            codes = keep.tile([P, SLOTS], U32, name=name + "_codes", tag=tag or name + "_codes", align_bytes=64)
+            scales = keep.tile([P, SLOTS], U8, name=name + "_scales", align_bytes=64)
+            nc.vector.quantize_mx(out=codes[:].bitcast(fmt), scales=scales[:], in_=src[:])
+            return codes, scales, fmt
+
+        def product(stationary, tile_nr, moving):
+            cols = slice(tile_nr * P, (tile_nr + 1) * P)
+            acc = bank()
+            nc.tensor.matmul_mx(
+                out=acc[:],
+                lhsT=stationary[0][:, cols].bitcast(stationary[2]),
+                lhsT_scale=stationary[1][:, cols],
+                rhs=moving[0][:].bitcast(moving[2]),
+                rhs_scale=moving[1][:],
+                start=True,
+                stop=True,
+            )
+            return acc
+
+        def woven_tile(name=None):
+            if name:
+                return keep.tile([P, SLOTS * PACK], BF16, name=name, tag=name, align_bytes=64)
+            return woven.tile([P, SLOTS * PACK], BF16, name="woven", align_bytes=64)
+
+        def weave_dealt(rows):
+            dst = woven_tile()
+            nc.scalar.copy(
+                out=dst[:].rearrange("p (r s t) -> p s t r", r=PACK, t=PACK),
+                in_=rows[:].rearrange("p (t s r) -> p s t r", t=PACK, r=PACK),
+            )
+            return dst
+
+        def weave_pair(dst, rows, h):
+            nc.scalar.copy(
+                out=dst[:].rearrange("p (i t) -> p i t", t=PACK)[:, :, 2 * h : 2 * h + 2],
+                in_=rows[:, 2 * h * SLOTS : (2 * h + 2) * SLOTS].rearrange("p (t i) -> p i t", t=2),
+            )
+
+        def turn(rows, name):
+            dst = woven_tile(name)
+            words = rows[:].bitcast(F32).rearrange("p (t s u) -> p t u s", t=PACK, u=2)
+            dst_words = dst[:].bitcast(F32).rearrange("s (t p u) -> s t p u", t=PACK, u=2)
+            for half in range(2):
+                acc = bank()
+                quarters = acc[:].rearrange("s (t u p) -> s t u p", t=2, u=2)
+                for t in range(2):
+                    for u in range(2):
+                        nc.tensor.transpose(quarters[:, t, u, :], words[:, 2 * half + t, u, :], ident[:])
+                nc.scalar.copy(
+                    out=dst_words[:, 2 * half : 2 * half + 2, :, :],
+                    in_=acc[:].rearrange("s (t u p) -> s t p u", t=2, u=2),
+                )
+            return dst
+
+        def load_row(name, src):
+            row = keep.tile([P, POOL // P], F32, name=name + "_row")
+            nc.scalar.dma_start(out=row[:], in_=src[0, :].rearrange("(p c) -> p c", p=P))
+            return row
+
+        def spread(name, row):
+            table = keep.tile([P, POOL], F32, name=name + "_table")
+            places = table[:].rearrange("m (p c) -> m p c", p=P)
+            for b in range(4):
+                acc = bank()
+                for cc in range(4):
+                    c = 4 * b + cc
+                    nc.tensor.transpose(
+                        acc[:, cc * P : (cc + 1) * P], row[:, c : c + 1].to_broadcast([P, P]), ident[:]
+                    )
+                nc.scalar.activation(
+                    out=places[:, :, 4 * b : 4 * b + 4],
+                    in_=acc[:].rearrange("m (c p) -> m p c", c=4),
+                    func=ACT.Copy,
+                )
+            return table
+
+        def pick(name, table, slot_list, tag=None):
+            picked = planes.tile([P, SLOTS], F32, name=name + "_picked", tag=tag or name + "_picked")
+            nc.vector.tensor_copy(out=picked[:], in_=table[:].indirect(slot_list[:]))
+            return picked
+
+        def to_columns(name, dealt, factor):
+            acc = bank()
+            for r in range(PACK):
+                nc.tensor.transpose(acc[:, r * P : (r + 1) * P], dealt[:, r, :], ident[:])
+            cols = keep.tile([P, PACK], F32, name=name + "_cols")
+            nc.scalar.activation(
+                out=cols[:], in_=acc[:].rearrange("s (r m) -> s r m", r=PACK)[:, :, 0], func=ACT.Copy, scale=factor
+            )
+            return cols
+
+        nc.sync.dma_start(q_list[:], qoffs)
+        q_planes = [load_plane(Q, 0)]
+        rows = {name: load_row(name, src) for name, src in (("ts", ts), ("sq", sq_), ("wq", wq), ("lse", lse), ("dl", dl))}
+        q_planes.append(load_plane(Q, 1))
+        nc.sync.dma_start(k_list[:], offs)
+        ident = keep.tile([P, P], F32, name="ident")
+        make_identity(nc, ident[:])
+        windows = [keep.tile([P, POOL], F32, name="window%d" % w) for w in range(4)]
+        for window in windows:
+            nc.vector.memset(window[:], 0.0)
+
+        q_rows = keep.tile([P, PACK * SLOTS], BF16, name="q_rows", align_bytes=64)
+        k_rows = keep.tile([P, PACK * SLOTS], BF16, name="k_rows", align_bytes=64)
+        do_rows = keep.tile([P, PACK * SLOTS], BF16, name="do_rows", align_bytes=64)
+        v_rows = keep.tile([P, 2 * SLOTS], BF16, name="v_rows", align_bytes=64)
+
+        def row_of(rows_tile, t):
+            return rows_tile[:, t * SLOTS : (t + 1) * SLOTS]
+
+        q_planes.extend(load_plane(Q, t) for t in (2, 3))
+        picked = {}
+        for t, name in enumerate((None, "ts", "sq", "wq")):
+            gather_plane(row_of(q_rows, t), q_planes[t], q_list)
+            if name:
+                picked[name] = pick(name, spread(name, rows[name]), k_list if name == "ts" else q_list)
+        gather_plane(row_of(k_rows, 0), load_plane(K, 0), k_list)
+        picked["lse"] = pick("lse", spread("lse", rows["lse"]), q_list)
+        dl_table = spread("dl", rows["dl"])
+        k_woven = woven_tile()
+        for t in range(1, PACK):
+            gather_plane(row_of(k_rows, t), load_plane(K, t), k_list)
+        ts_row = picked["ts"]
+        q_d = quantize("q_d", weave_dealt(q_rows), E4M3)
+        q_turned = turn(q_rows, "q_turned")
+        ts_cols = to_columns("ts", ts_row[:].rearrange("m (c i) -> m c i", c=PACK), 1.0)
+        sq_cols = to_columns("sq", picked["sq"][:].rearrange("m (s r) -> m r s", r=PACK), 1.0)
+        wq_cols = to_columns("wq", picked["wq"][:].rearrange("m (s r) -> m r s", r=PACK), 1.0)
+        neg_lse_cols = to_columns("lse", picked["lse"][:].rearrange("m (s r) -> m r s", r=PACK), -1.0)
+        gate_cols = keep.tile([P, PACK], F32, name="gate_cols")
+        nc.vector.tensor_tensor(out=gate_cols[:], in0=wq_cols[:], in1=sq_cols[:], op=ALU.mult)
+        for h in range(2):
+            weave_pair(k_woven, k_rows, h)
+        picked["dl"] = pick("dl", dl_table, q_list, slot_of(K, 3))
+
+        for t in range(PACK):
+            gather_plane(row_of(do_rows, t), load_plane(DO, t), q_list)
+        v_woven = woven_tile("v_woven")
+        v_places = v_woven[:].rearrange("p (i t) -> p i t", t=PACK)
+        for t in range(2):
+            gather_plane(row_of(v_rows, t), load_plane(V, t), k_list)
+        for t in range(2, PACK):
+            gather_plane(v_places[:, :, t], load_plane(V, t), k_list)
+
+        k_d = quantize("k_d", k_woven, E4M3)
+        prob = keep.tile([P, PACK * SLOTS], F32, name="prob")
+        weight = planes.tile([P, PACK * SLOTS], F32, name="weight", tag=slot_of(DO, 3))
+        scaled = [bank() for r in range(PACK)]
+        for c in range(PACK):
+            scores = product(k_d, c, q_d)
+            by_key = pairs.tile([P, SLOTS], F32, name="by_key")
+            nc.scalar.activation(out=by_key[:], in_=scores[:], func=ACT.Copy, scale=ts_cols[:, c : c + 1])
+            for r in range(PACK):
+                nc.tensor.transpose(scaled[r][:, c * P : (c + 1) * P], by_key[:, r * P : (r + 1) * P], ident[:])
+        for r in range(PACK):
+            nc.scalar.activation(
+                out=row_of(prob, r), in_=scaled[r][:], func=ACT.Exp, bias=neg_lse_cols[:, r : r + 1], scale=sq_cols[:, r : r + 1]
+            )
+            nc.vector.scalar_tensor_tensor(
+                out=row_of(weight, r), in0=row_of(prob, r), scalar=gate_cols[:, r : r + 1], in1=ts_row[:],
+                op0=ALU.mult, op1=ALU.mult,
+            )
+
+        do_e = quantize("do_e", weave_dealt(do_rows), E5M2)
+        weave_pair(v_woven, v_rows, 0)
+        k_turned = turn(k_rows, "k_turned")
+        dl_cols = to_columns("dl", picked["dl"][:].rearrange("m (s r) -> m r s", r=PACK), 1.0)
+        v_e = quantize("v_e", v_woven, E4M3)
+        q_j = quantize("q_j", q_turned, E4M3, tag="v_woven")
+
+        g_rows = keep.tile([P, PACK * SLOTS], BF16, name="g_rows", align_bytes=64)
+        for r in range(PACK):
+            dp = product(do_e, r, v_e)
+            nc.vector.scalar_tensor_tensor(
+                out=row_of(g_rows, r), in0=dp[:], scalar=dl_cols[:, r : r + 1], in1=row_of(weight, r),
+                op0=ALU.subtract, op1=ALU.mult,
+            )
+
+        g_woven = woven_tile()
+        nc.vector.tensor_copy(
+            out=g_woven[:].rearrange("p (c i t) -> p c t i", i=PACK, t=PACK),
+            in_=g_rows[:].rearrange("p (t c i) -> p c t i", t=PACK, i=PACK),
+        )
+        g_j = quantize("g_j", g_woven, E5M2)
+        g_i = quantize("g_i", turn(g_rows, "g_turned"), E5M2)
+        k_i = quantize("k_i", k_turned, E4M3, tag="g_turned")
+
+        def put(acc_view, window, slot_list, out, t):
+            result = staged.tile([P, SLOTS], F32, name="result")
+            nc.scalar.copy(out=result[:].rearrange("p (s r) -> p s r", r=PACK), in_=acc_view)
+            nc.vector.tensor_copy(out=window[:].indirect(slot_list[:]), in_=result[:])
+            nc.sync.dma_start(out=out.rearrange("(p t) n -> t p n", t=PACK)[t], in_=window[:])
+
+        for half in range(2):
+            for w in range(2):
+                t = 2 * half + w
+                dk = product(q_j, t, g_j)
+                put(dk[:].rearrange("p (s r) -> p s r", r=PACK), windows[w], k_list, out_1, t)
+            for w in range(2):
+                t = 2 * half + w
+                dq = product(k_i, t, g_i)
+                put(dq[:].rearrange("p (r s) -> p s r", r=PACK), windows[2 + w], q_list, out_0, t)

@@ -19,7 +19,7 @@ ALU = mybir.AluOpType
 
 P = 128
 PACK = 4
-RING = 7
+RING = 5
 Q, K, DO, V = range(4)
 
 
@@ -33,10 +33,10 @@ def tile_attend_gclatt_qk_kernel(
         woven = ctx.enter_context(tc.tile_pool(name="woven", bufs=3))
         pairs = ctx.enter_context(tc.tile_pool(name="pairs", bufs=4))
         staged = ctx.enter_context(tc.tile_pool(name="staged", bufs=4))
-        psum = ctx.enter_context(tc.psum_pool(name="psum", bufs=8))
+        psum = ctx.enter_context(tc.psum_pool(name="psum", bufs=1))
 
-        def bank():
-            return psum.tile([P, SLOTS], F32, name="bank")
+        def bank(nr):
+            return psum.tile([P, SLOTS], F32, name="bank", tag="bank%d" % nr)
 
         q_list = keep.tile([P, SLOTS // 16], U16, name="q_list")
         k_list = keep.tile([P, SLOTS // 16], U16, name="k_list")
@@ -46,22 +46,22 @@ def tile_attend_gclatt_qk_kernel(
 
         def load_plane(src_nr, t):
             src = (qT, kT, doT, vT)[src_nr]
-            plane = planes.tile([P, POOL], F32, name="plane", tag=slot_of(src_nr, t))
+            plane = planes.tile([P, POOL], F32, name="plane", tag=slot_of(src_nr, t), align_bytes=64)
             nc.sync.dma_start(out=plane[:], in_=src.rearrange("(p t) n -> t p n", t=PACK)[t])
             return plane
 
         def gather_plane(dst, plane, slot_list):
             nc.vector.tensor_copy(out=dst, in_=plane[:].indirect(slot_list[:]))
 
-        def quantize(name, src, fmt, tag=None):
-            codes = keep.tile([P, SLOTS], U32, name=name + "_codes", tag=tag or name + "_codes", align_bytes=64)
+        def quantize(name, src, fmt, tag=None, pool=keep):
+            codes = pool.tile([P, SLOTS], U32, name=name + "_codes", tag=tag or name + "_codes", align_bytes=64)
             scales = keep.tile([P, SLOTS], U8, name=name + "_scales", align_bytes=64)
             nc.vector.quantize_mx(out=codes[:].bitcast(fmt), scales=scales[:], in_=src[:])
             return codes, scales, fmt
 
-        def product(stationary, tile_nr, moving):
+        def product(stationary, tile_nr, moving, bank_nr):
             cols = slice(tile_nr * P, (tile_nr + 1) * P)
-            acc = bank()
+            acc = bank(bank_nr)
             nc.tensor.matmul_mx(
                 out=acc[:],
                 lhsT=stationary[0][:, cols].bitcast(stationary[2]),
@@ -86,22 +86,22 @@ def tile_attend_gclatt_qk_kernel(
             )
             return dst
 
-        def weave_pair(dst, rows, h):
-            nc.scalar.copy(
+        def weave_pair(copy, dst, two_rows, h):
+            copy(
                 out=dst[:].rearrange("p (i t) -> p i t", t=PACK)[:, :, 2 * h : 2 * h + 2],
-                in_=rows[:, 2 * h * SLOTS : (2 * h + 2) * SLOTS].rearrange("p (t i) -> p i t", t=2),
+                in_=two_rows.rearrange("p (t i) -> p i t", t=2),
             )
 
-        def turn(rows, name):
+        def turn(halves, name, first_bank):
             dst = woven_tile(name)
-            words = rows[:].bitcast(F32).rearrange("p (t s u) -> p t u s", t=PACK, u=2)
             dst_words = dst[:].bitcast(F32).rearrange("s (t p u) -> s t p u", t=PACK, u=2)
             for half in range(2):
-                acc = bank()
+                words = halves[half].bitcast(F32).rearrange("p (t s u) -> p t u s", t=2, u=2)
+                acc = bank(first_bank + half)
                 quarters = acc[:].rearrange("s (t u p) -> s t u p", t=2, u=2)
                 for t in range(2):
                     for u in range(2):
-                        nc.tensor.transpose(quarters[:, t, u, :], words[:, 2 * half + t, u, :], ident[:])
+                        nc.tensor.transpose(quarters[:, t, u, :], words[:, t, u, :], ident[:])
                 nc.scalar.copy(
                     out=dst_words[:, 2 * half : 2 * half + 2, :, :],
                     in_=acc[:].rearrange("s (t u p) -> s t p u", t=2, u=2),
@@ -117,7 +117,7 @@ def tile_attend_gclatt_qk_kernel(
             table = keep.tile([P, POOL], F32, name=name + "_table")
             places = table[:].rearrange("m (p c) -> m p c", p=P)
             for b in range(4):
-                acc = bank()
+                acc = bank(b)
                 for cc in range(4):
                     c = 4 * b + cc
                     nc.tensor.transpose(
@@ -130,13 +130,18 @@ def tile_attend_gclatt_qk_kernel(
                 )
             return table
 
+        def by_partition(name, picked):
+            cols = keep.tile([P, PACK], F32, name=name + "_cols")
+            nc.sync.dma_start(out=cols[:], in_=picked[0:1, :].rearrange("o (s r) -> o s r", r=PACK))
+            return cols
+
         def pick(name, table, slot_list, tag=None):
             picked = planes.tile([P, SLOTS], F32, name=name + "_picked", tag=tag or name + "_picked")
             nc.vector.tensor_copy(out=picked[:], in_=table[:].indirect(slot_list[:]))
             return picked
 
         def to_columns(name, dealt, factor):
-            acc = bank()
+            acc = bank(4)
             for r in range(PACK):
                 nc.tensor.transpose(acc[:, r * P : (r + 1) * P], dealt[:, r, :], ident[:])
             cols = keep.tile([P, PACK], F32, name=name + "_cols")
@@ -154,7 +159,7 @@ def tile_attend_gclatt_qk_kernel(
         make_identity(nc, ident[:])
         windows = [keep.tile([P, POOL], F32, name="window%d" % w) for w in range(4)]
         for window in windows:
-            nc.vector.memset(window[:], 0.0)
+            nc.vector.memset(window[:].bitcast(U32), 0)
 
         q_rows = keep.tile([P, PACK * SLOTS], BF16, name="q_rows", align_bytes=64)
         k_rows = keep.tile([P, PACK * SLOTS], BF16, name="k_rows", align_bytes=64)
@@ -164,30 +169,29 @@ def tile_attend_gclatt_qk_kernel(
         def row_of(rows_tile, t):
             return rows_tile[:, t * SLOTS : (t + 1) * SLOTS]
 
+        def halves_of(rows_tile):
+            return [rows_tile[:, 2 * h * SLOTS : (2 * h + 2) * SLOTS] for h in range(2)]
+
         q_planes.extend(load_plane(Q, t) for t in (2, 3))
-        picked = {}
+        picked, cols = {}, {}
         for t, name in enumerate((None, "ts", "sq", "wq")):
             gather_plane(row_of(q_rows, t), q_planes[t], q_list)
             if name:
                 picked[name] = pick(name, spread(name, rows[name]), k_list if name == "ts" else q_list)
+            if name in ("sq", "wq"):
+                cols[name] = by_partition(name, picked[name])
         gather_plane(row_of(k_rows, 0), load_plane(K, 0), k_list)
-        picked["lse"] = pick("lse", spread("lse", rows["lse"]), q_list)
-        dl_table = spread("dl", rows["dl"])
+        lse_cols = by_partition("lse", pick("lse", spread("lse", rows["lse"]), q_list))
+        sq_cols, wq_cols = cols["sq"], cols["wq"]
         k_woven = woven_tile()
         for t in range(1, PACK):
             gather_plane(row_of(k_rows, t), load_plane(K, t), k_list)
         ts_row = picked["ts"]
         q_d = quantize("q_d", weave_dealt(q_rows), E4M3)
-        q_turned = turn(q_rows, "q_turned")
         ts_cols = to_columns("ts", ts_row[:].rearrange("m (c i) -> m c i", c=PACK), 1.0)
-        sq_cols = to_columns("sq", picked["sq"][:].rearrange("m (s r) -> m r s", r=PACK), 1.0)
-        wq_cols = to_columns("wq", picked["wq"][:].rearrange("m (s r) -> m r s", r=PACK), 1.0)
-        neg_lse_cols = to_columns("lse", picked["lse"][:].rearrange("m (s r) -> m r s", r=PACK), -1.0)
-        gate_cols = keep.tile([P, PACK], F32, name="gate_cols")
-        nc.vector.tensor_tensor(out=gate_cols[:], in0=wq_cols[:], in1=sq_cols[:], op=ALU.mult)
         for h in range(2):
-            weave_pair(k_woven, k_rows, h)
-        picked["dl"] = pick("dl", dl_table, q_list, slot_of(K, 3))
+            weave_pair(nc.scalar.copy, k_woven, halves_of(k_rows)[h], h)
+        dl_cols = by_partition("dl", pick("dl", spread("dl", rows["dl"]), q_list))
 
         for t in range(PACK):
             gather_plane(row_of(do_rows, t), load_plane(DO, t), q_list)
@@ -195,15 +199,21 @@ def tile_attend_gclatt_qk_kernel(
         v_places = v_woven[:].rearrange("p (i t) -> p i t", t=PACK)
         for t in range(2):
             gather_plane(row_of(v_rows, t), load_plane(V, t), k_list)
+        weave_pair(nc.scalar.copy, v_woven, v_rows[:], 0)
         for t in range(2, PACK):
-            gather_plane(v_places[:, :, t], load_plane(V, t), k_list)
+            last = load_plane(V, t)
+            gather_plane(v_places[:, :, t], last, k_list)
 
         k_d = quantize("k_d", k_woven, E4M3)
+        neg_lse_cols = keep.tile([P, PACK], F32, name="neg_lse_cols")
+        nc.scalar.activation(out=neg_lse_cols[:], in_=lse_cols[:], func=ACT.Copy, scale=-1.0)
+        gate_cols = keep.tile([P, PACK], F32, name="gate_cols")
+        nc.vector.tensor_tensor(out=gate_cols[:], in0=wq_cols[:], in1=sq_cols[:], op=ALU.mult)
         prob = keep.tile([P, PACK * SLOTS], F32, name="prob")
-        weight = planes.tile([P, PACK * SLOTS], F32, name="weight", tag=slot_of(DO, 3))
-        scaled = [bank() for r in range(PACK)]
+        weight = planes.tile([P, PACK * SLOTS], F32, name="weight", tag=slot_of(DO, 3), align_bytes=64)
+        scaled = [bank(4 + r) for r in range(PACK)]
         for c in range(PACK):
-            scores = product(k_d, c, q_d)
+            scores = product(k_d, c, q_d, c)
             by_key = pairs.tile([P, SLOTS], F32, name="by_key")
             nc.scalar.activation(out=by_key[:], in_=scores[:], func=ACT.Copy, scale=ts_cols[:, c : c + 1])
             for r in range(PACK):
@@ -217,28 +227,25 @@ def tile_attend_gclatt_qk_kernel(
                 op0=ALU.mult, op1=ALU.mult,
             )
 
-        do_e = quantize("do_e", weave_dealt(do_rows), E5M2)
-        weave_pair(v_woven, v_rows, 0)
-        k_turned = turn(k_rows, "k_turned")
-        dl_cols = to_columns("dl", picked["dl"][:].rearrange("m (s r) -> m r s", r=PACK), 1.0)
+        do_e = quantize("do_e", weave_dealt(do_rows), E5M2, slot_of(V, 1), planes)
+        q_turned = turn(halves_of(q_rows), "q_turned", 4)
+        k_turned = turn(halves_of(k_rows), "k_turned", 6)
         v_e = quantize("v_e", v_woven, E4M3)
         q_j = quantize("q_j", q_turned, E4M3, tag="v_woven")
 
-        g_rows = keep.tile([P, PACK * SLOTS], BF16, name="g_rows", align_bytes=64)
+        g_halves = [keep.tile([P, 2 * SLOTS], BF16, name="g_half%d" % h, align_bytes=64)[:] for h in range(2)]
         for r in range(PACK):
-            dp = product(do_e, r, v_e)
+            dp = product(do_e, r, v_e, r)
             nc.vector.scalar_tensor_tensor(
-                out=row_of(g_rows, r), in0=dp[:], scalar=dl_cols[:, r : r + 1], in1=row_of(weight, r),
+                out=row_of(g_halves[r // 2], r % 2), in0=dp[:], scalar=dl_cols[:, r : r + 1], in1=row_of(weight, r),
                 op0=ALU.subtract, op1=ALU.mult,
             )
 
         g_woven = woven_tile()
-        nc.vector.tensor_copy(
-            out=g_woven[:].rearrange("p (c i t) -> p c t i", i=PACK, t=PACK),
-            in_=g_rows[:].rearrange("p (t c i) -> p c t i", t=PACK, i=PACK),
-        )
+        weave_pair(nc.scalar.copy, g_woven, g_halves[0], 0)
+        weave_pair(nc.vector.tensor_copy, g_woven, g_halves[1], 1)
         g_j = quantize("g_j", g_woven, E5M2)
-        g_i = quantize("g_i", turn(g_rows, "g_turned"), E5M2)
+        g_i = quantize("g_i", turn(g_halves, "g_turned", 4), E5M2)
         k_i = quantize("k_i", k_turned, E4M3, tag="g_turned")
 
         def put(acc_view, window, slot_list, out, t):
@@ -250,9 +257,9 @@ def tile_attend_gclatt_qk_kernel(
         for half in range(2):
             for w in range(2):
                 t = 2 * half + w
-                dk = product(q_j, t, g_j)
+                dk = product(q_j, t, g_j, t)
                 put(dk[:].rearrange("p (s r) -> p s r", r=PACK), windows[w], k_list, out_1, t)
             for w in range(2):
                 t = 2 * half + w
-                dq = product(k_i, t, g_i)
+                dq = product(k_i, t, g_i, 4 + t)
                 put(dq[:].rearrange("p (r s) -> p s r", r=PACK), windows[2 + w], q_list, out_0, t)

@@ -81,8 +81,18 @@ def tile_attend_gclatt_qk_kernel(
         def weave_dealt(rows):
             dst = woven_tile()
             nc.scalar.copy(
-                out=dst[:].rearrange("p (r s t) -> p s t r", r=PACK, t=PACK),
-                in_=rows[:].rearrange("p (t s r) -> p s t r", t=PACK, r=PACK),
+                out=dst[:].rearrange("p (r s t) -> p r s t", r=PACK, t=PACK),
+                in_=rows[:].rearrange("p (t s r) -> p r s t", t=PACK, r=PACK),
+            )
+            return dst
+
+        def in_slot(name, src_nr, t):
+            return planes.tile([P, SLOTS * PACK], BF16, name=name, tag=slot_of(src_nr, t), align_bytes=64)
+
+        def weave(rows):
+            dst = woven_tile()
+            nc.scalar.copy(
+                out=dst[:].rearrange("p (i t) -> p i t", t=PACK), in_=rows[:].rearrange("p (t i) -> p i t", t=PACK)
             )
             return dst
 
@@ -92,8 +102,7 @@ def tile_attend_gclatt_qk_kernel(
                 in_=two_rows.rearrange("p (t i) -> p i t", t=2),
             )
 
-        def turn(halves, name, first_bank):
-            dst = woven_tile(name)
+        def turn(halves, dst, first_bank):
             dst_words = dst[:].bitcast(F32).rearrange("s (t p u) -> s t p u", t=PACK, u=2)
             for half in range(2):
                 words = halves[half].bitcast(F32).rearrange("p (t s u) -> p t u s", t=2, u=2)
@@ -187,7 +196,7 @@ def tile_attend_gclatt_qk_kernel(
         for t in range(1, PACK):
             gather_plane(row_of(k_rows, t), load_plane(K, t), k_list)
         ts_row = picked["ts"]
-        q_d = quantize("q_d", weave_dealt(q_rows), E4M3)
+        q_d = quantize("q_d", weave(q_rows), E4M3)
         ts_cols = to_columns("ts", ts_row[:].rearrange("m (c i) -> m c i", c=PACK), 1.0)
         for h in range(2):
             weave_pair(nc.scalar.copy, k_woven, halves_of(k_rows)[h], h)
@@ -215,7 +224,12 @@ def tile_attend_gclatt_qk_kernel(
         for c in range(PACK):
             scores = product(k_d, c, q_d, c)
             by_key = pairs.tile([P, SLOTS], F32, name="by_key")
-            nc.scalar.activation(out=by_key[:], in_=scores[:], func=ACT.Copy, scale=ts_cols[:, c : c + 1])
+            nc.scalar.activation(
+                out=by_key[:].rearrange("p (r s) -> p r s", r=PACK),
+                in_=scores[:].rearrange("p (s r) -> p r s", r=PACK),
+                func=ACT.Copy,
+                scale=ts_cols[:, c : c + 1],
+            )
             for r in range(PACK):
                 nc.tensor.transpose(scaled[r][:, c * P : (c + 1) * P], by_key[:, r * P : (r + 1) * P], ident[:])
         for r in range(PACK):
@@ -227,9 +241,9 @@ def tile_attend_gclatt_qk_kernel(
                 op0=ALU.mult, op1=ALU.mult,
             )
 
-        do_e = quantize("do_e", weave_dealt(do_rows), E5M2, slot_of(V, 1), planes)
-        q_turned = turn(halves_of(q_rows), "q_turned", 4)
-        k_turned = turn(halves_of(k_rows), "k_turned", 6)
+        do_e = quantize("do_e", weave_dealt(do_rows), E5M2, slot_of(V, 2), planes)
+        q_turned = turn(halves_of(q_rows), in_slot("q_turned", V, 1), 4)
+        k_turned = turn(halves_of(k_rows), in_slot("k_turned", V, 3), 6)
         v_e = quantize("v_e", v_woven, E4M3)
         q_j = quantize("q_j", q_turned, E4M3, tag="v_woven")
 
@@ -245,7 +259,7 @@ def tile_attend_gclatt_qk_kernel(
         weave_pair(nc.scalar.copy, g_woven, g_halves[0], 0)
         weave_pair(nc.vector.tensor_copy, g_woven, g_halves[1], 1)
         g_j = quantize("g_j", g_woven, E5M2)
-        g_i = quantize("g_i", turn(g_halves, "g_turned", 4), E5M2)
+        g_i = quantize("g_i", turn(g_halves, woven_tile("g_turned"), 4), E5M2)
         k_i = quantize("k_i", k_turned, E4M3, tag="g_turned")
 
         def put(acc_view, window, slot_list, out, t):

@@ -19,7 +19,7 @@ ALU = mybir.AluOpType
 
 P = 128
 PACK = 4
-RING = 5
+RING = 6
 Q, K, DO, V = range(4)
 
 
@@ -30,7 +30,7 @@ def tile_attend_gclatt_qk_kernel(
     with ExitStack() as ctx:
         keep = ctx.enter_context(tc.tile_pool(name="keep", bufs=1))
         planes = ctx.enter_context(tc.tile_pool(name="planes", bufs=1))
-        woven = ctx.enter_context(tc.tile_pool(name="woven", bufs=3))
+        woven = ctx.enter_context(tc.tile_pool(name="woven", bufs=2))
         pairs = ctx.enter_context(tc.tile_pool(name="pairs", bufs=4))
         staged = ctx.enter_context(tc.tile_pool(name="staged", bufs=4))
         psum = ctx.enter_context(tc.psum_pool(name="psum", bufs=1))
@@ -89,12 +89,10 @@ def tile_attend_gclatt_qk_kernel(
         def in_slot(name, src_nr, t):
             return planes.tile([P, SLOTS * PACK], BF16, name=name, tag=slot_of(src_nr, t), align_bytes=64)
 
-        def weave(rows):
-            dst = woven_tile()
+        def weave(rows, dst):
             nc.scalar.copy(
                 out=dst[:].rearrange("p (i t) -> p i t", t=PACK), in_=rows[:].rearrange("p (t i) -> p i t", t=PACK)
             )
-            return dst
 
         def weave_pair(copy, dst, two_rows, h):
             copy(
@@ -117,16 +115,29 @@ def tile_attend_gclatt_qk_kernel(
                 )
             return dst
 
+        def turn_woven(src, dst, first_bank):
+            words = src[:].bitcast(F32).rearrange("p (s r h) -> p h r s", r=PACK, h=2)
+            places = dst[:].rearrange("s (t p r) -> s t p r", t=PACK, r=PACK)
+            for h in range(2):
+                acc = bank(first_bank + h)
+                for r in range(PACK):
+                    nc.tensor.transpose(acc[:, r * P : (r + 1) * P], words[:, h, r, :], ident[:])
+                nc.scalar.copy(
+                    out=places[:, 2 * h : 2 * h + 2, :, :],
+                    in_=acc[:].bitcast(BF16).rearrange("s (r p e) -> s e p r", r=PACK, e=2),
+                )
+            return dst
+
         def load_row(name, src):
             row = keep.tile([P, POOL // P], F32, name=name + "_row")
             nc.scalar.dma_start(out=row[:], in_=src[0, :].rearrange("(p c) -> p c", p=P))
             return row
 
-        def spread(name, row):
+        def spread(name, row, first_bank=0):
             table = keep.tile([P, POOL], F32, name=name + "_table")
             places = table[:].rearrange("m (p c) -> m p c", p=P)
             for b in range(4):
-                acc = bank(b)
+                acc = bank(first_bank + b)
                 for cc in range(4):
                     c = 4 * b + cc
                     nc.tensor.transpose(
@@ -139,25 +150,21 @@ def tile_attend_gclatt_qk_kernel(
                 )
             return table
 
-        def by_partition(name, picked):
-            cols = keep.tile([P, PACK], F32, name=name + "_cols")
-            nc.sync.dma_start(out=cols[:], in_=picked[0:1, :].rearrange("o (s r) -> o s r", r=PACK))
-            return cols
-
         def pick(name, table, slot_list, tag=None):
             picked = planes.tile([P, SLOTS], F32, name=name + "_picked", tag=tag or name + "_picked")
             nc.vector.tensor_copy(out=picked[:], in_=table[:].indirect(slot_list[:]))
             return picked
 
-        def to_columns(name, dealt, factor):
-            acc = bank(4)
+        def to_columns(cols, parts, bank_nr, factor):
+            acc = bank(bank_nr)
             for r in range(PACK):
-                nc.tensor.transpose(acc[:, r * P : (r + 1) * P], dealt[:, r, :], ident[:])
-            cols = keep.tile([P, PACK], F32, name=name + "_cols")
+                nc.tensor.transpose(acc[:, r * P : (r + 1) * P], parts[:, r, :], ident[:])
             nc.scalar.activation(
-                out=cols[:], in_=acc[:].rearrange("s (r m) -> s r m", r=PACK)[:, :, 0], func=ACT.Copy, scale=factor
+                out=cols, in_=acc[:].rearrange("s (r m) -> s r m", r=PACK)[:, :, 0], func=ACT.Copy, scale=factor
             )
-            return cols
+
+        def dealt(picked):
+            return picked[:].rearrange("m (s r) -> m r s", r=PACK)
 
         nc.sync.dma_start(q_list[:], qoffs)
         q_planes = [load_plane(Q, 0)]
@@ -168,12 +175,13 @@ def tile_attend_gclatt_qk_kernel(
         make_identity(nc, ident[:])
         windows = [keep.tile([P, POOL], F32, name="window%d" % w) for w in range(4)]
         for window in windows:
-            nc.vector.memset(window[:].bitcast(U32), 0)
+            for half in range(2):
+                nc.gpsimd.memset(window[:, half * POOL // 2 : (half + 1) * POOL // 2], 0.0)
 
-        q_rows = keep.tile([P, PACK * SLOTS], BF16, name="q_rows", align_bytes=64)
-        k_rows = keep.tile([P, PACK * SLOTS], BF16, name="k_rows", align_bytes=64)
-        do_rows = keep.tile([P, PACK * SLOTS], BF16, name="do_rows", align_bytes=64)
-        v_rows = keep.tile([P, 2 * SLOTS], BF16, name="v_rows", align_bytes=64)
+        q_rows = keep.tile([P, PACK * SLOTS], F32, name="q_rows")
+        k_rows = keep.tile([P, PACK * SLOTS], F32, name="k_rows", tag="k_rows")
+        do_rows = keep.tile([P, PACK * SLOTS], F32, name="do_rows")
+        v_rows = keep.tile([P, 2 * SLOTS], F32, name="v_rows", tag="v_rows")
 
         def row_of(rows_tile, t):
             return rows_tile[:, t * SLOTS : (t + 1) * SLOTS]
@@ -182,25 +190,33 @@ def tile_attend_gclatt_qk_kernel(
             return [rows_tile[:, 2 * h * SLOTS : (2 * h + 2) * SLOTS] for h in range(2)]
 
         q_planes.extend(load_plane(Q, t) for t in (2, 3))
-        picked, cols = {}, {}
+        picked = {}
         for t, name in enumerate((None, "ts", "sq", "wq")):
             gather_plane(row_of(q_rows, t), q_planes[t], q_list)
             if name:
                 picked[name] = pick(name, spread(name, rows[name]), k_list if name == "ts" else q_list)
-            if name in ("sq", "wq"):
-                cols[name] = by_partition(name, picked[name])
         gather_plane(row_of(k_rows, 0), load_plane(K, 0), k_list)
-        lse_cols = by_partition("lse", pick("lse", spread("lse", rows["lse"]), q_list))
-        sq_cols, wq_cols = cols["sq"], cols["wq"]
-        k_woven = woven_tile()
-        for t in range(1, PACK):
+        picked["lse"] = pick("lse", spread("lse", rows["lse"]), q_list)
+        gather_plane(row_of(k_rows, 1), load_plane(K, 1), k_list)
+        k_woven = woven_tile("k_woven")
+        for t in range(2, PACK):
             gather_plane(row_of(k_rows, t), load_plane(K, t), k_list)
         ts_row = picked["ts"]
-        q_d = quantize("q_d", weave(q_rows), E4M3)
-        ts_cols = to_columns("ts", ts_row[:].rearrange("m (c i) -> m c i", c=PACK), 1.0)
+        q_woven = woven_tile("q_woven")
+        weave(q_rows, q_woven)
+        q_d = quantize("q_d", q_woven, E4M3)
         for h in range(2):
             weave_pair(nc.scalar.copy, k_woven, halves_of(k_rows)[h], h)
-        dl_cols = by_partition("dl", pick("dl", spread("dl", rows["dl"]), q_list))
+        dl_table = spread("dl", rows["dl"], 4)
+        late = keep.tile([P, SLOTS + 4 * PACK], F32, name="late", tag="k_rows")
+        ts_cols, sq_cols, wq_cols, neg_lse_cols = (late[:, SLOTS + n * PACK : SLOTS + (n + 1) * PACK] for n in range(4))
+        to_columns(ts_cols, ts_row[:].rearrange("m (c i) -> m c i", c=PACK), 0, 1.0)
+        to_columns(sq_cols, dealt(picked["sq"]), 1, 1.0)
+        to_columns(wq_cols, dealt(picked["wq"]), 2, 1.0)
+        to_columns(neg_lse_cols, dealt(picked["lse"]), 3, -1.0)
+        k_d = quantize("k_d", k_woven, E4M3)
+        picked["dl"] = late[:, 0:SLOTS]
+        nc.vector.tensor_copy(out=picked["dl"], in_=dl_table[:].indirect(q_list[:]))
 
         for t in range(PACK):
             gather_plane(row_of(do_rows, t), load_plane(DO, t), q_list)
@@ -213,11 +229,8 @@ def tile_attend_gclatt_qk_kernel(
             last = load_plane(V, t)
             gather_plane(v_places[:, :, t], last, k_list)
 
-        k_d = quantize("k_d", k_woven, E4M3)
-        neg_lse_cols = keep.tile([P, PACK], F32, name="neg_lse_cols")
-        nc.scalar.activation(out=neg_lse_cols[:], in_=lse_cols[:], func=ACT.Copy, scale=-1.0)
         gate_cols = keep.tile([P, PACK], F32, name="gate_cols")
-        nc.vector.tensor_tensor(out=gate_cols[:], in0=wq_cols[:], in1=sq_cols[:], op=ALU.mult)
+        nc.vector.tensor_tensor(out=gate_cols[:], in0=wq_cols, in1=sq_cols, op=ALU.mult)
         prob = keep.tile([P, PACK * SLOTS], F32, name="prob")
         weight = planes.tile([P, PACK * SLOTS], F32, name="weight", tag=slot_of(DO, 3), align_bytes=64)
         scaled = [bank(4 + r) for r in range(PACK)]
@@ -242,8 +255,10 @@ def tile_attend_gclatt_qk_kernel(
             )
 
         do_e = quantize("do_e", weave_dealt(do_rows), E5M2, slot_of(V, 2), planes)
-        q_turned = turn(halves_of(q_rows), in_slot("q_turned", V, 1), 4)
-        k_turned = turn(halves_of(k_rows), in_slot("k_turned", V, 3), 6)
+        dl_cols = keep.tile([P, PACK], F32, name="dl_cols", tag="v_rows")
+        to_columns(dl_cols[:], dealt(picked["dl"]), 3, 1.0)
+        q_turned = turn_woven(q_woven, in_slot("q_turned", V, 1), 4)
+        k_turned = turn_woven(k_woven, in_slot("k_turned", V, 3), 6)
         v_e = quantize("v_e", v_woven, E4M3)
         q_j = quantize("q_j", q_turned, E4M3, tag="v_woven")
 

from contextlib import ExitStack

import concourse.mybir as mybir
from concourse.masks import make_identity

D, SLOTS, POOL = 512, 512, 2048
FLOPS = 4 * 2 * 512 * 512 * 512
BYTES = 6 * D * POOL * 4 + 5 * POOL * 4 + 2 * 128 * 32 * 2

F32 = mybir.dt.float32
BF16 = mybir.dt.bfloat16
U32 = mybir.dt.uint32
U16 = mybir.dt.uint16
U8 = mybir.dt.uint8
E4M3 = mybir.dt.float8_e4m3fn_x4
E5M2 = mybir.dt.float8_e5m2_x4
ACT = mybir.ActivationFunctionType
ALU = mybir.AluOpType

P = 128
PACK = 4
RING = 6
Q, K, DO, V = range(4)


def tile_attend_gclatt_qk_kernel(
    tc, qT, kT, doT, vT, sq_, ts, lse, dl, wq, qoffs, offs, out_0, out_1
):
    nc = tc.nc
    with ExitStack() as ctx:
        keep = ctx.enter_context(tc.tile_pool(name="keep", bufs=1))
        planes = ctx.enter_context(tc.tile_pool(name="planes", bufs=1))
        woven = ctx.enter_context(tc.tile_pool(name="woven", bufs=2))
        pairs = ctx.enter_context(tc.tile_pool(name="pairs", bufs=4))
        staged = ctx.enter_context(tc.tile_pool(name="staged", bufs=4))
        psum = ctx.enter_context(tc.psum_pool(name="psum", bufs=1))

        def bank(nr):
            return psum.tile([P, SLOTS], F32, name="bank", tag="bank%d" % nr)

        q_list = keep.tile([P, SLOTS // 16], U16, name="q_list")
        k_list = keep.tile([P, SLOTS // 16], U16, name="k_list")

        def slot_of(src_nr, t):
            return "slot%d" % ((PACK * src_nr + t) % RING)

        def load_plane(src_nr, t):
            src = (qT, kT, doT, vT)[src_nr]
            plane = planes.tile([P, POOL], F32, name="plane", tag=slot_of(src_nr, t), align_bytes=64)
            nc.sync.dma_start(out=plane[:], in_=src.rearrange("(p t) n -> t p n", t=PACK)[t])
            return plane

        def gather_plane(dst, plane, slot_list):
            nc.vector.tensor_copy(out=dst, in_=plane[:].indirect(slot_list[:]))

        def quantize(name, src, fmt, tag=None, pool=keep):
            codes = pool.tile([P, SLOTS], U32, name=name + "_codes", tag=tag or name + "_codes", align_bytes=64)
            scales = keep.tile([P, SLOTS], U8, name=name + "_scales", align_bytes=64)
            nc.vector.quantize_mx(out=codes[:].bitcast(fmt), scales=scales[:], in_=src[:])
            return codes, scales, fmt

        def product(stationary, tile_nr, moving, bank_nr):
            cols = slice(tile_nr * P, (tile_nr + 1) * P)
            acc = bank(bank_nr)
            nc.tensor.matmul_mx(
                out=acc[:],
                lhsT=stationary[0][:, cols].bitcast(stationary[2]),
                lhsT_scale=stationary[1][:, cols],
                rhs=moving[0][:].bitcast(moving[2]),
                rhs_scale=moving[1][:],
                start=True,
                stop=True,
            )
            return acc

        def woven_tile(name=None):
            if name:
                return keep.tile([P, SLOTS * PACK], BF16, name=name, tag=name, align_bytes=64)
            return woven.tile([P, SLOTS * PACK], BF16, name="woven", align_bytes=64)

        def weave_dealt(rows):
            dst = woven_tile()
            nc.scalar.copy(
                out=dst[:].rearrange("p (r s t) -> p r s t", r=PACK, t=PACK),
                in_=rows[:].rearrange("p (t s r) -> p r s t", t=PACK, r=PACK),
            )
            return dst

        def in_slot(name, src_nr, t):
            return planes.tile([P, SLOTS * PACK], BF16, name=name, tag=slot_of(src_nr, t), align_bytes=64)

        def weave(rows, dst):
            nc.scalar.copy(
                out=dst[:].rearrange("p (i t) -> p i t", t=PACK), in_=rows[:].rearrange("p (t i) -> p i t", t=PACK)
            )

        def weave_pair(copy, dst, two_rows, h):
            copy(
                out=dst[:].rearrange("p (i t) -> p i t", t=PACK)[:, :, 2 * h : 2 * h + 2],
                in_=two_rows.rearrange("p (t i) -> p i t", t=2),
            )

        def turn(halves, dst, first_bank):
            dst_words = dst[:].bitcast(F32).rearrange("s (t p u) -> s t p u", t=PACK, u=2)
            for half in range(2):
                words = halves[half].bitcast(F32).rearrange("p (t s u) -> p t u s", t=2, u=2)
                acc = bank(first_bank + half)
                quarters = acc[:].rearrange("s (t u p) -> s t u p", t=2, u=2)
                for t in range(2):
                    for u in range(2):
                        nc.tensor.transpose(quarters[:, t, u, :], words[:, t, u, :], ident[:])
                nc.scalar.copy(
                    out=dst_words[:, 2 * half : 2 * half + 2, :, :],
                    in_=acc[:].rearrange("s (t u p) -> s t p u", t=2, u=2),
                )
            return dst

        def turn_woven(src, dst, first_bank):
            words = src[:].bitcast(F32).rearrange("p (s r h) -> p h r s", r=PACK, h=2)
            places = dst[:].rearrange("s (t p r) -> s t p r", t=PACK, r=PACK)
            for h in range(2):
                acc = bank(first_bank + h)
                for r in range(PACK):
                    nc.tensor.transpose(acc[:, r * P : (r + 1) * P], words[:, h, r, :], ident[:])
                nc.scalar.copy(
                    out=places[:, 2 * h : 2 * h + 2, :, :],
                    in_=acc[:].bitcast(BF16).rearrange("s (r p e) -> s e p r", r=PACK, e=2),
                )
            return dst

        def load_row(name, src):
            row = keep.tile([P, POOL // P], F32, name=name + "_row")
            nc.scalar.dma_start(out=row[:], in_=src[0, :].rearrange("(p c) -> p c", p=P))
            return row

        def spread(name, row, first_bank=0):
            table = keep.tile([P, POOL], F32, name=name + "_table")
            places = table[:].rearrange("m (p c) -> m p c", p=P)
            for b in range(4):
                acc = bank(first_bank + b)
                for cc in range(4):
                    c = 4 * b + cc
                    nc.tensor.transpose(
                        acc[:, cc * P : (cc + 1) * P], row[:, c : c + 1].to_broadcast([P, P]), ident[:]
                    )
                nc.scalar.activation(
                    out=places[:, :, 4 * b : 4 * b + 4],
                    in_=acc[:].rearrange("m (c p) -> m p c", c=4),
                    func=ACT.Copy,
                )
            return table

        def pick(name, table, slot_list, tag=None):
            picked = planes.tile([P, SLOTS], F32, name=name + "_picked", tag=tag or name + "_picked")
            nc.vector.tensor_copy(out=picked[:], in_=table[:].indirect(slot_list[:]))
            return picked

        def to_columns(cols, parts, bank_nr, factor):
            acc = bank(bank_nr)
            for r in range(PACK):
                nc.tensor.transpose(acc[:, r * P : (r + 1) * P], parts[:, r, :], ident[:])
            nc.scalar.activation(
                out=cols, in_=acc[:].rearrange("s (r m) -> s r m", r=PACK)[:, :, 0], func=ACT.Copy, scale=factor
            )

        def dealt(picked):
            return picked[:].rearrange("m (s r) -> m r s", r=PACK)

        nc.sync.dma_start(q_list[:], qoffs)
        q_planes = [load_plane(Q, 0)]
        rows = {name: load_row(name, src) for name, src in (("ts", ts), ("sq", sq_), ("wq", wq), ("lse", lse), ("dl", dl))}
        q_planes.append(load_plane(Q, 1))
        nc.sync.dma_start(k_list[:], offs)
        ident = keep.tile([P, P], F32, name="ident")
        make_identity(nc, ident[:])
        windows = [keep.tile([P, POOL], F32, name="window%d" % w) for w in range(4)]
        for window in windows:
            for half in range(2):
                nc.gpsimd.memset(window[:, half * POOL // 2 : (half + 1) * POOL // 2], 0.0)

        q_rows = keep.tile([P, PACK * SLOTS], F32, name="q_rows")
        k_rows = keep.tile([P, PACK * SLOTS], F32, name="k_rows", tag="k_rows")
        do_rows = keep.tile([P, PACK * SLOTS], F32, name="do_rows")
        v_rows = keep.tile([P, 2 * SLOTS], F32, name="v_rows", tag="v_rows")

        def row_of(rows_tile, t):
            return rows_tile[:, t * SLOTS : (t + 1) * SLOTS]

        def halves_of(rows_tile):
            return [rows_tile[:, 2 * h * SLOTS : (2 * h + 2) * SLOTS] for h in range(2)]

        q_planes.extend(load_plane(Q, t) for t in (2, 3))
        picked = {}
        for t, name in enumerate((None, "ts", "sq", "wq")):
            gather_plane(row_of(q_rows, t), q_planes[t], q_list)
            if name:
                picked[name] = pick(name, spread(name, rows[name]), k_list if name == "ts" else q_list)
        gather_plane(row_of(k_rows, 0), load_plane(K, 0), k_list)
        picked["lse"] = pick("lse", spread("lse", rows["lse"]), q_list)
        gather_plane(row_of(k_rows, 1), load_plane(K, 1), k_list)
        k_woven = woven_tile("k_woven")
        for t in range(2, PACK):
            gather_plane(row_of(k_rows, t), load_plane(K, t), k_list)
        ts_row = picked["ts"]
        q_woven = woven_tile("q_woven")
        weave(q_rows, q_woven)
        q_d = quantize("q_d", q_woven, E4M3)
        for h in range(2):
            weave_pair(nc.scalar.copy, k_woven, halves_of(k_rows)[h], h)
        dl_table = spread("dl", rows["dl"], 4)
        late = keep.tile([P, SLOTS + 4 * PACK], F32, name="late", tag="k_rows")
        ts_cols, sq_cols, wq_cols, neg_lse_cols = (late[:, SLOTS + n * PACK : SLOTS + (n + 1) * PACK] for n in range(4))
        to_columns(ts_cols, ts_row[:].rearrange("m (c i) -> m c i", c=PACK), 0, 1.0)
        to_columns(sq_cols, dealt(picked["sq"]), 1, 1.0)
        to_columns(wq_cols, dealt(picked["wq"]), 2, 1.0)
        to_columns(neg_lse_cols, dealt(picked["lse"]), 3, -1.0)
        k_d = quantize("k_d", k_woven, E4M3)
        picked["dl"] = late[:, 0:SLOTS]
        nc.vector.tensor_copy(out=picked["dl"], in_=dl_table[:].indirect(q_list[:]))

        for t in range(PACK):
            gather_plane(row_of(do_rows, t), load_plane(DO, t), q_list)
        v_woven = woven_tile("v_woven")
        v_places = v_woven[:].rearrange("p (i t) -> p i t", t=PACK)
        for t in range(2):
            gather_plane(row_of(v_rows, t), load_plane(V, t), k_list)
        weave_pair(nc.scalar.copy, v_woven, v_rows[:], 0)
        for t in range(2, PACK):
            last = load_plane(V, t)
            gather_plane(v_places[:, :, t], last, k_list)

        gate_cols = keep.tile([P, PACK], F32, name="gate_cols")
        nc.vector.tensor_tensor(out=gate_cols[:], in0=wq_cols, in1=sq_cols, op=ALU.mult)
        prob = keep.tile([P, PACK * SLOTS], F32, name="prob")
        weight = planes.tile([P, PACK * SLOTS], F32, name="weight", tag=slot_of(DO, 3), align_bytes=64)
        scaled = [bank(4 + r) for r in range(PACK)]
        for c in range(PACK):
            scores = product(k_d, c, q_d, c)
            by_key = pairs.tile([P, SLOTS], F32, name="by_key")
            nc.scalar.activation(
                out=by_key[:].rearrange("p (r s) -> p r s", r=PACK),
                in_=scores[:].rearrange("p (s r) -> p r s", r=PACK),
                func=ACT.Copy,
                scale=ts_cols[:, c : c + 1],
            )
            for r in range(PACK):
                nc.tensor.transpose(scaled[r][:, c * P : (c + 1) * P], by_key[:, r * P : (r + 1) * P], ident[:])
        for r in range(PACK):
            nc.scalar.activation(
                out=row_of(prob, r), in_=scaled[r][:], func=ACT.Exp, bias=neg_lse_cols[:, r : r + 1], scale=sq_cols[:, r : r + 1]
            )
            nc.vector.scalar_tensor_tensor(
                out=row_of(weight, r), in0=row_of(prob, r), scalar=gate_cols[:, r : r + 1], in1=ts_row[:],
                op0=ALU.mult, op1=ALU.mult,
            )

        do_e = quantize("do_e", weave_dealt(do_rows), E5M2, slot_of(V, 2), planes)
        dl_cols = keep.tile([P, PACK], F32, name="dl_cols", tag="v_rows")
        to_columns(dl_cols[:], dealt(picked["dl"]), 3, 1.0)
        q_turned = turn_woven(q_woven, in_slot("q_turned", V, 1), 4)
        k_turned = turn_woven(k_woven, in_slot("k_turned", V, 3), 6)
        v_e = quantize("v_e", v_woven, E4M3)
        q_j = quantize("q_j", q_turned, E4M3, tag="v_woven")

        g_halves = [keep.tile([P, 2 * SLOTS], BF16, name="g_half%d" % h, align_bytes=64)[:] for h in range(2)]
        for r in range(PACK):
            dp = product(do_e, r, v_e, r)
            nc.vector.scalar_tensor_tensor(
                out=row_of(g_halves[r // 2], r % 2), in0=dp[:], scalar=dl_cols[:, r : r + 1], in1=row_of(weight, r),
                op0=ALU.subtract, op1=ALU.mult,
            )

        g_woven = woven_tile()
        weave_pair(nc.scalar.copy, g_woven, g_halves[0], 0)
        weave_pair(nc.vector.tensor_copy, g_woven, g_halves[1], 1)
        g_j = quantize("g_j", g_woven, E5M2)
        g_i = quantize("g_i", turn(g_halves, woven_tile("g_turned"), 4), E5M2)
        k_i = quantize("k_i", k_turned, E4M3, tag="g_turned")

        def put(acc_view, window, slot_list, out, t):
            result = staged.tile([P, SLOTS], F32, name="result")
            nc.scalar.copy(out=result[:].rearrange("p (s r) -> p s r", r=PACK), in_=acc_view)
            nc.vector.tensor_copy(out=window[:].indirect(slot_list[:]), in_=result[:])
            nc.sync.dma_start(out=out.rearrange("(p t) n -> t p n", t=PACK)[t], in_=window[:])

        for half in range(2):
            for w in range(2):
                t = 2 * half + w
                dk = product(q_j, t, g_j, t)
                put(dk[:].rearrange("p (s r) -> p s r", r=PACK), windows[w], k_list, out_1, t)
            for w in range(2):
                t = 2 * half + w
                dq = product(k_i, t, g_i, 4 + t)
                put(dq[:].rearrange("p (r s) -> p s r", r=PACK), windows[2 + w], q_list, out_0, t)
